import numpy as np, ml_dtypes
CORES = [31,71,111]
N = 3
DEG, TK = 2, 256
MASK = [[2,0],[2,1],[2,0]]
def setup_inputs(rng):
    return {"x": rng.standard_normal((N, 128, TK), dtype=np.float32).astype(ml_dtypes.bfloat16), "w": rng.standard_normal((N, 128, DEG * 128), dtype=np.float32).astype(ml_dtypes.bfloat16)}
def setup_inputs_big(rng):
    d = setup_inputs(rng)
    for k in ("x", "w"): d[k] = (d[k].astype(np.float32) * 1024.0).astype(d[k].dtype)
    return d
def setup_inputs_small(rng):
    d = setup_inputs(rng)
    for k in ("x", "w"): d[k] = (d[k].astype(np.float32) * (1 / 1024.0)).astype(d[k].dtype)
    return d
def setup_inputs_apart(rng):
    d = setup_inputs(rng)
    f = (10.0 ** rng.permutation(np.linspace(-1.5, 1.5, N))).astype(np.float32).reshape(N, 1, 1)
    for k in ("x", "w"): d[k] = (d[k].astype(np.float32) * f).astype(d[k].dtype)
    return d
def reference(x, w):
    X, W = x.astype(np.float64), w.astype(np.float64)
    y = np.zeros((N, 128, TK))
    for r in range(N):
        for i, j in enumerate(MASK[r]):
            y[r] += W[r][:, 128 * i:128 * i + 128].T @ X[j]
    return {"y": y.astype(ml_dtypes.bfloat16 if x.dtype != np.float64 else np.float64)}

@@ -1,0 +1,80 @@
+from concourse.bass import DstId, RemoteDMATransfer
+
+SCRATCH = {
+    "xd": ("dram", [128, 256], "bfloat16"),
+    "xs": ("sbuf", [128, 256], "bfloat16"),
+    "ws": ("sbuf", [128, 256], "bfloat16"),
+    "land0": ("sbuf", [128, 256], "bfloat16"),
+    "land1": ("sbuf", [128, 256], "bfloat16"),
+    "land2": ("sbuf", [128, 256], "bfloat16"),
+    "acc": ("psum", [128, 256], "float32"),
+    "ys": ("sbuf", [128, 256], "bfloat16"),
+}
+SEMAPHORES = ["staged", "xin", "win", "sent", "arr0", "arr1", "arr2", "mm", "cp", "stored"]
+
+
+def _plan(owner, T, topo):
+    mask_tab = T.tables["MASK"]
+    src = T.cores[owner]
+    cons = [q for q in range(len(T.cores)) if q != owner and owner in mask_tab[q]]
+    if not cons:
+        return []
+    common = -1
+    for q in cons:
+        assert topo.may_write(src, T.cores[q])
+        common &= topo.mask(src, T.cores[q])
+    bits = [e for e in range(16) if (common >> e) & 1]
+    per = 1
+    while per * 2 * len(cons) <= len(bits):
+        per *= 2
+    out = []
+    for k, q in enumerate(cons):
+        m = 0
+        for e in bits[k * per:(k + 1) * per]:
+            m |= 1 << e
+        out.append((q, m, per))
+    return out
+
+
+def rank_program(g, core, T, topo):
+    rank = T.rank_of(core)
+    if rank is None:
+        return
+    need = T.tables["MASK"][rank]
+    sends = _plan(rank, T, topo)
+
+    if sends:
+        g.sync.dma_start(T.xd[:], T.x[:]).then_inc(T.sem.staged, 16)
+    g.sync.dma_start(T.ws[:], T.w[:]).then_inc(T.sem.win, 16)
+    if rank in need:
+        g.sync.dma_start(T.xs[:], T.x[:]).then_inc(T.sem.xin, 16)
+
+    if sends:
+        g.wait_ge(T.sem.staged, 16)
+        trs = []
+        for q, m, per in sends:
+            rid, pid, _se = topo.addr(T.cores[q])
+            trs.append(RemoteDMATransfer(dst_ids=[DstId(rid=rid, pnc=pid)], dma_engine_mask=m,
+                                         remote_sem=T.sem["arr%d" % rank], src=T.xd[:], dst=T["land%d" % rank][:]))
+        g.remote_dma_fused(trs, local_sem=T.sem.sent)
+        g.wait_ge(T.sem.sent, sum(per for _q, _m, per in sends))
+
+    order = [i for i, j in enumerate(need) if j == rank] + [i for i, j in enumerate(need) if j != rank]
+    g.tensor.wait_ge(T.sem.win, 16)
+    for n, i in enumerate(order):
+        j = need[i]
+        if j == rank:
+            g.tensor.wait_ge(T.sem.xin, 16)
+            rhs = T.xs[:]
+        else:
+            per = [p for q, _m, p in _plan(j, T, topo) if q == rank][0]
+            g.tensor.wait_ge(T.sem["arr%d" % j], per)
+            rhs = T["land%d" % j][:]
+        mmi = g.tensor.matmul(T.acc[:], T.ws[:, 128 * i:128 * i + 128], rhs, n == 0, n == len(order) - 1)
+    mmi.then_inc(T.sem.mm, 1)
+
+    g.vector.wait_ge(T.sem.mm, 1)
+    g.vector.tensor_copy(T.ys[:], T.acc[:]).then_inc(T.sem.cp, 1)
+    g.scalar.wait_ge(T.sem.cp, 1)
+    g.scalar.dma_start(T.y[:], T.ys[:]).then_inc(T.sem.stored, 16)
+    g.scalar.wait_ge(T.sem.stored, 16)

@@ -1,5 +1,3 @@
-from concourse.bass import DstId, RemoteDMATransfer
-
 SCRATCH = {
     "xd": ("dram", [128, 256], "bfloat16"),
     "xs": ("sbuf", [128, 256], "bfloat16"),
@@ -7,10 +5,10 @@ SCRATCH = {
     "land0": ("sbuf", [128, 256], "bfloat16"),
     "land1": ("sbuf", [128, 256], "bfloat16"),
     "land2": ("sbuf", [128, 256], "bfloat16"),
-    "acc": ("psum", [128, 256], "float32"),
+    "acc": ("psum", [128, 1024], "float32"),
     "ys": ("sbuf", [128, 256], "bfloat16"),
 }
-SEMAPHORES = ["staged", "xin", "win", "sent", "arr0", "arr1", "arr2", "mm", "cp", "stored"]
+SEMAPHORES = ["staged", "xin", "win", "sent", "arr0", "arr1", "arr2", "mm0", "mm1", "cp0", "cp1", "stored0", "stored1"]
 
 
 def _plan(owner, T, topo):
@@ -19,20 +17,29 @@ def _plan(owner, T, topo):
     cons = [q for q in range(len(T.cores)) if q != owner and owner in mask_tab[q]]
     if not cons:
         return []
+
+    def hops(q):
+        a, b = topo.chip(src), topo.chip(T.cores[q])
+        if a == b:
+            return 0
+        return 1 if topo.mates(a, b) or topo.same_plane(a, b) else 2
+
+    cons.sort(key=lambda q: -hops(q))
     common = -1
     for q in cons:
         assert topo.may_write(src, T.cores[q])
         common &= topo.mask(src, T.cores[q])
     bits = [e for e in range(16) if (common >> e) & 1]
-    per = 1
-    while per * 2 * len(cons) <= len(bits):
-        per *= 2
+    slots = 2
+    while slots < len(cons):
+        slots *= 2
     out = []
     for k, q in enumerate(cons):
+        mine = bits[k::slots]
         m = 0
-        for e in bits[k * per:(k + 1) * per]:
+        for e in mine:
             m |= 1 << e
-        out.append((q, m, per))
+        out.append((q, m, len(mine)))
     return out
 
 
@@ -42,6 +49,8 @@ def rank_program(g, core, T, topo):
         return
     need = T.tables["MASK"][rank]
     sends = _plan(rank, T, topo)
+    cols = [slice(0, 128), slice(128, 256)]
+    bank = [slice(0, 128), slice(512, 640)]
 
     if sends:
         g.sync.dma_start(T.xd[:], T.x[:]).then_inc(T.sem.staged, 16)
@@ -51,30 +60,35 @@ def rank_program(g, core, T, topo):
 
     if sends:
         g.wait_ge(T.sem.staged, 16)
-        trs = []
         for q, m, per in sends:
             rid, pid, _se = topo.addr(T.cores[q])
-            trs.append(RemoteDMATransfer(dst_ids=[DstId(rid=rid, pnc=pid)], dma_engine_mask=m,
-                                         remote_sem=T.sem["arr%d" % rank], src=T.xd[:], dst=T["land%d" % rank][:]))
-        g.remote_dma_fused(trs, local_sem=T.sem.sent)
+            g.remote_dma(T["land%d" % rank][:], T.xd[:], T.sem["arr%d" % rank], T.sem.sent, pid, rid, m)
         g.wait_ge(T.sem.sent, sum(per for _q, _m, per in sends))
 
-    order = [i for i, j in enumerate(need) if j == rank] + [i for i, j in enumerate(need) if j != rank]
+    own = [i for i, j in enumerate(need) if j == rank]
+    far = [i for i, j in enumerate(need) if j != rank]
     g.tensor.wait_ge(T.sem.win, 16)
-    for n, i in enumerate(order):
+    if own:
+        g.tensor.wait_ge(T.sem.xin, 16)
+    for h in range(2):
+        for n, i in enumerate(own):
+            mmi = g.tensor.matmul(T.acc[:, bank[h]], T.ws[:, 128 * i:128 * i + 128], T.xs[:, cols[h]],
+                                  n == 0, not far and n == len(own) - 1)
+        if own and not far:
+            mmi.then_inc(T.sem["mm%d" % h], 1)
+    for i in far:
         j = need[i]
-        if j == rank:
-            g.tensor.wait_ge(T.sem.xin, 16)
-            rhs = T.xs[:]
-        else:
-            per = [p for q, _m, p in _plan(j, T, topo) if q == rank][0]
-            g.tensor.wait_ge(T.sem["arr%d" % j], per)
-            rhs = T["land%d" % j][:]
-        mmi = g.tensor.matmul(T.acc[:], T.ws[:, 128 * i:128 * i + 128], rhs, n == 0, n == len(order) - 1)
-    mmi.then_inc(T.sem.mm, 1)
+        g.tensor.wait_ge(T.sem["arr%d" % j], [p for q, _m, p in _plan(j, T, topo) if q == rank][0])
+    for h in range(2):
+        for n, i in enumerate(far):
+            mmi = g.tensor.matmul(T.acc[:, bank[h]], T.ws[:, 128 * i:128 * i + 128], T["land%d" % need[i]][:, cols[h]],
+                                  not own and n == 0, n == len(far) - 1)
+        if far:
+            mmi.then_inc(T.sem["mm%d" % h], 1)
 
-    g.vector.wait_ge(T.sem.mm, 1)
-    g.vector.tensor_copy(T.ys[:], T.acc[:]).then_inc(T.sem.cp, 1)
-    g.scalar.wait_ge(T.sem.cp, 1)
-    g.scalar.dma_start(T.y[:], T.ys[:]).then_inc(T.sem.stored, 16)
-    g.scalar.wait_ge(T.sem.stored, 16)
+    for h, q in enumerate([g.scalar, g.sync]):
+        g.vector.wait_ge(T.sem["mm%d" % h], 1)
+        g.vector.tensor_copy(T.ys[:, cols[h]], T.acc[:, bank[h]]).then_inc(T.sem["cp%d" % h], 1)
+        q.wait_ge(T.sem["cp%d" % h], 1)
+        q.dma_start(T.y[:, cols[h]], T.ys[:, cols[h]]).then_inc(T.sem["stored%d" % h], 16)
+        q.wait_ge(T.sem["stored%d" % h], 16)

SCRATCH = {
    "xd": ("dram", [128, 256], "bfloat16"),
    "xs": ("sbuf", [128, 256], "bfloat16"),
    "ws": ("sbuf", [128, 256], "bfloat16"),
    "land0": ("sbuf", [128, 256], "bfloat16"),
    "land1": ("sbuf", [128, 256], "bfloat16"),
    "land2": ("sbuf", [128, 256], "bfloat16"),
    "acc": ("psum", [128, 1024], "float32"),
    "ys": ("sbuf", [128, 256], "bfloat16"),
}
SEMAPHORES = ["staged", "xin", "win", "sent", "arr0", "arr1", "arr2", "mm0", "mm1", "cp0", "cp1", "stored0", "stored1"]


def _plan(owner, T, topo):
    mask_tab = T.tables["MASK"]
    src = T.cores[owner]
    cons = [q for q in range(len(T.cores)) if q != owner and owner in mask_tab[q]]
    if not cons:
        return []

    def hops(q):
        a, b = topo.chip(src), topo.chip(T.cores[q])
        if a == b:
            return 0
        return 1 if topo.mates(a, b) or topo.same_plane(a, b) else 2

    cons.sort(key=lambda q: -hops(q))
    common = -1
    for q in cons:
        assert topo.may_write(src, T.cores[q])
        common &= topo.mask(src, T.cores[q])
    bits = [e for e in range(16) if (common >> e) & 1]
    slots = 2
    while slots < len(cons):
        slots *= 2
    out = []
    for k, q in enumerate(cons):
        mine = bits[k::slots]
        m = 0
        for e in mine:
            m |= 1 << e
        out.append((q, m, len(mine)))
    return out


def rank_program(g, core, T, topo):
    rank = T.rank_of(core)
    if rank is None:
        return
    need = T.tables["MASK"][rank]
    sends = _plan(rank, T, topo)
    cols = [slice(0, 128), slice(128, 256)]
    bank = [slice(0, 128), slice(512, 640)]

    if sends:
        g.sync.dma_start(T.xd[:], T.x[:]).then_inc(T.sem.staged, 16)
    g.sync.dma_start(T.ws[:], T.w[:]).then_inc(T.sem.win, 16)
    if rank in need:
        g.sync.dma_start(T.xs[:], T.x[:]).then_inc(T.sem.xin, 16)

    if sends:
        g.wait_ge(T.sem.staged, 16)
        for q, m, per in sends:
            rid, pid, _se = topo.addr(T.cores[q])
            g.remote_dma(T["land%d" % rank][:], T.xd[:], T.sem["arr%d" % rank], T.sem.sent, pid, rid, m)
        g.wait_ge(T.sem.sent, sum(per for _q, _m, per in sends))

    own = [i for i, j in enumerate(need) if j == rank]
    far = [i for i, j in enumerate(need) if j != rank]
    g.tensor.wait_ge(T.sem.win, 16)
    if own:
        g.tensor.wait_ge(T.sem.xin, 16)
    for h in range(2):
        for n, i in enumerate(own):
            mmi = g.tensor.matmul(T.acc[:, bank[h]], T.ws[:, 128 * i:128 * i + 128], T.xs[:, cols[h]],
                                  n == 0, not far and n == len(own) - 1)
        if own and not far:
            mmi.then_inc(T.sem["mm%d" % h], 1)
    for i in far:
        j = need[i]
        g.tensor.wait_ge(T.sem["arr%d" % j], [p for q, _m, p in _plan(j, T, topo) if q == rank][0])
    for h in range(2):
        for n, i in enumerate(far):
            mmi = g.tensor.matmul(T.acc[:, bank[h]], T.ws[:, 128 * i:128 * i + 128], T["land%d" % need[i]][:, cols[h]],
                                  not own and n == 0, n == len(far) - 1)
        if far:
            mmi.then_inc(T.sem["mm%d" % h], 1)

    for h, q in enumerate([g.scalar, g.sync]):
        g.vector.wait_ge(T.sem["mm%d" % h], 1)
        g.vector.tensor_copy(T.ys[:, cols[h]], T.acc[:, bank[h]]).then_inc(T.sem["cp%d" % h], 1)
        q.wait_ge(T.sem["cp%d" % h], 1)
        q.dma_start(T.y[:, cols[h]], T.ys[:, cols[h]]).then_inc(T.sem["stored%d" % h], 16)
        q.wait_ge(T.sem["stored%d" % h], 16)
